import numpy as np
import ml_dtypes


def mxq(x, axis, fmt="e4m3"):
    dtype, down = {"e4m3": (ml_dtypes.float8_e4m3fn, 7), "e5m2": (ml_dtypes.float8_e5m2, 14)}[fmt]
    v = np.moveaxis(np.asarray(x, np.float32).astype(ml_dtypes.bfloat16).astype(np.float64), axis, -1)
    blocks = v.reshape(v.shape[:-1] + (-1, 32))
    amax = np.abs(blocks).max(-1, keepdims=True)
    byte = np.maximum(np.where(amax > 0, np.frexp(amax)[1] - 1 + 127, 0) - down, 1)
    scale = np.exp2(byte - 127.0)
    codes = (blocks / scale).astype(np.float32).astype(dtype).astype(np.float64)
    return np.moveaxis((codes * scale).reshape(v.shape), -1, axis)


WIDE = False


def mx_kscale(k):
    if not WIDE:
        return np.ones(k)
    levels = np.array([10, -10, 5, -5, 0])
    if k % 512:
        return np.exp2(np.random.permutation(np.resize(levels, k // 32))).repeat(32)
    a = np.empty((k // 512, 16))
    for p in range(k // 512):
        a[p, :8] = np.random.permutation(np.resize(levels, 8))
        for g in range(8):
            far = levels[np.abs(levels - a[p, g]) >= 10]
            a[p, g + 8] = far[np.random.randint(len(far))]
    return np.exp2(a.ravel()).repeat(32)


BF16 = ml_dtypes.bfloat16


def bf(x):
    return np.asarray(x, np.float32).astype(BF16)


def f64(x):
    return np.asarray(x).astype(np.float64)


M, K, J, F, D, C = 1024, 1024, 3, 1024, 512, 1024


def draw0():
    s, u = mx_kscale(K), mx_kscale(D)
    t = mx_kscale(F)
    amp = F ** -0.25
    tj = np.tile(t, J)
    return {"x": bf(np.random.standard_normal((M, K)) * s),
            "w": bf(np.random.standard_normal((K, J * F)) * amp / np.sqrt(K) / s[:, None] * tj),
            "b": bf(0.3 * np.random.standard_normal(J * F) * amp * tj),
            "e": bf(np.random.standard_normal((C, D)) * u),
            "g": bf(np.random.standard_normal((D, F)) * amp / np.sqrt(D) / u[:, None] / t),
            "a": bf(0.3 * np.random.standard_normal(F) * amp / t),
            "r": bf(1 + 0.1 * np.random.standard_normal(C)),
            "d": bf(0.3 * np.random.standard_normal(C))}


def core(x, w, b, e, g, a, r, d):
    z = (mxq(f64(x), 1, "e4m3") @ mxq(f64(w), 0, "e4m3")) + f64(b)
    h = np.max(z.reshape(M, J, F), axis=1)
    v = (mxq(f64(e), 1, "e4m3") @ mxq(f64(g), 0, "e4m3")) + f64(a)
    y = mxq(h, 1, "e4m3") @ mxq(v, 1, "e4m3").T
    return y * f64(r) + f64(d)


def e4m3fn_bytes(y):
    return np.clip(np.asarray(y, np.float64), -448.0, 448.0).astype(np.float32).astype(ml_dtypes.float8_e4m3fn).view(np.uint8)


def e4m3fn_values(b):
    return np.asarray(b, np.uint8).view(ml_dtypes.float8_e4m3fn).astype(np.float64)


def setup_inputs():
    d = draw0()
    x0 = np.asarray(d['x']).astype(np.float64)
    s = (np.max(np.abs(x0), axis=(0,), keepdims=True) / 448.0).astype(np.float32)
    out = {}
    for k, v in d.items():
        if k == 'x':
            out['x_bytes'] = e4m3fn_bytes(x0 / s.astype(np.float64))
            out['x_scale'] = s
        else:
            out[k] = v
    return out


def reference(x_bytes, x_scale, w, b, e, g, a, r, d):
    return core(e4m3fn_values(x_bytes) * x_scale.astype(np.float64), w, b, e, g, a, r, d)

from contextlib import ExitStack

import concourse.mybir as mybir
from concourse.masks import make_identity

M, K, J, F, D, C = 1024, 1024, 3, 1024, 512, 1024
FLOPS = 2 * M * K * J * F + 2 * C * D * F + 2 * M * F * C

P = 128
F32 = mybir.dt.float32
BF16 = mybir.dt.bfloat16
U8 = mybir.dt.uint8
U32 = mybir.dt.uint32
FP8 = mybir.dt.float8_e4m3fn
FP8X4 = mybir.dt.float8_e4m3fn_x4
ADD = mybir.AluOpType.add
MULT = mybir.AluOpType.mult
MAX = mybir.AluOpType.max
IDENTITY = mybir.ActivationFunctionType.Identity

W_VEC = [[1, 3], [1, 2], [1, 2], [4, 2], [2, 0], [2, 0]]
G_VEC = [3, 3]
V_VEC = [True, True, True, True]
V_OUT_VEC = [1]
E_AT = 13
X_AT = 20
G_AT = 8
V_AT = [20, 24, 23, 27]
Y_AT = [36, 36, 35, 41]
YT_AT = [38, 42, 41, 49]
H_LAG = [1, 3]
X_LAG = [4, 4]
W_AT = [0, 1, 3, 5, 14]
W_LAG = 2
X1_AT = [1, 3, 9, 12]
Z_ORDER = [[0, 0], [1, 0], [2, 0], [3, 0], [4, 0], [5, 0], [0, 1], [1, 1], [2, 1], [3, 1], [4, 1], [5, 1]]
ADD_GP = [[0, 1, 1, 1], [1, 0, 1, 1]]


def tile_maxout_generated_head_f5_kernel(tc, x_bytes, x_scale, w, b, e, g, a, r, d, out):
    nc = tc.nc
    with ExitStack() as ctx:
        keep = ctx.enter_context(tc.tile_pool(name="keep", bufs=1))
        work = ctx.enter_context(tc.tile_pool(name="work", bufs=2))
        psum = ctx.enter_context(tc.psum_pool(name="psum", bufs=8))

        def kept(name, shape, dtype):
            return keep.tile(shape, dtype, name=name, align_bytes=64)

        def new_bank():
            bank = psum.tile([P, 512], F32, name="bank")
            return bank

        xs = kept("xs", [P, K], F32)
        x_raw = [kept(f"x_raw{h}", [P, 4, K], U8) for h in range(2)]
        x_bf = {}
        x_grp = {}
        x_codes = [kept(f"x_codes{h}", [P, 2, 512], U32) for h in range(2)]
        x_scales = [kept(f"x_scales{h}", [P, 2, 512], U8) for h in range(2)]
        w_codes = [[kept(f"w_codes{c}_{q}", [P, 512], U32) for q in range(2)] for c in range(6)]
        w_scales = [[kept(f"w_scales{c}_{q}", [P, 512], U8) for q in range(2)] for c in range(6)]
        e_raw = kept("e_raw", [P, 8, D], BF16)
        e_grp = {}
        e_codes = kept("e_codes", [P, C], U32)
        e_scales = kept("e_scales", [P, C], U8)
        g_raw = kept("g_raw", [P, 4, F], BF16)
        g_codes = [kept(f"g_codes{q}", [P, 512], U32) for q in range(2)]
        g_scales = [kept(f"g_scales{q}", [P, 512], U8) for q in range(2)]
        v_codes = [[kept(f"v_codes{q}_{n}", [P, 512], U32) for n in range(2)] for q in range(2)]
        v_scales = [[kept(f"v_scales{q}_{n}", [P, 512], U8) for n in range(2)] for q in range(2)]
        h_codes = [[kept(f"h_codes{q}_{h}", [P, 512], U32) for h in range(2)] for q in range(2)]
        h_scales = [[kept(f"h_scales{q}_{h}", [P, 512], U8) for h in range(2)] for q in range(2)]
        r_all = kept("r_all", [P, C], BF16)
        d_all = kept("d_all", [P, C], BF16)
        bias_rows = kept("bias_rows", [P, P], BF16)
        bias = kept("bias", [P, 48], F32)
        ident = kept("ident", [P, P], F32)
        ident_bf = kept("ident_bf", [P, P], BF16)
        warm = kept("warm", [P, 2], F32)

        w_raw = {}

        def load_w(c, q):
            group, piece = c // 3, c % 3
            t = work.tile([P, 4, 512], BF16, name="w_raw", bufs=5, align_bytes=64)
            col = piece * F + group * 512
            nc.sync.dma_start(
                out=t[:],
                in_=w[q * 512 : (q + 1) * 512, col : col + 512].rearrange("(p s) n -> p s n", s=4),
            )
            w_raw[c, q] = t

        x_rows = x_bytes.rearrange("(p i) k -> p i k", i=8)

        def load_x(h, i0, i1):
            nc.sync.dma_start(out=x_raw[h][:, i0:i1, :], in_=x_rows[:, 4 * h + i0 : 4 * h + i1, :])

        nc.scalar.dma_start(out=xs[:], in_=x_scale.rearrange("o k -> (o k)").partition_broadcast(P))
        load_x(0, 0, 1)
        load_x(0, 1, 4)
        load_w(0, 0)
        load_w(0, 1)
        nc.vector.memset(warm[:], 0.0)
        nc.scalar.activation(out=warm[:, 0:1], in_=warm[:, 1:2], func=IDENTITY)
        nc.gpsimd.memset(bias_rows[:], 0.0)
        make_identity(nc, ident[:])
        make_identity(nc, ident_bf[:])
        for c in range(8):
            row = b[c * 512 : (c + 1) * 512] if c < 6 else a[(c - 6) * 512 : (c - 5) * 512]
            nc.scalar.dma_start(
                out=bias_rows[4 * c : 4 * c + 4, :].rearrange("t (B i) -> t B i", i=8),
                in_=row.rearrange("(B t i) -> t B i", t=4, i=8),
            )

        for row, vec in ((32, r), (40, d)):
            nc.scalar.dma_start(out=bias_rows[row : row + 8, :], in_=vec.rearrange("(n p) -> n p", p=P))

        def copy(engine, out, in_):
            if engine == "v":
                nc.vector.tensor_copy(out=out, in_=in_)
            else:
                nc.scalar.copy(out=out, in_=in_)

        def x_product(h, i):
            t = work.tile([P, K], BF16, name="x_bf", bufs=3, align_bytes=64)
            x_bf[h, i] = t
            nc.vector.tensor_tensor(out=t[:], in0=x_raw[h][:, i, :].bitcast(FP8), in1=xs[:], op=MULT)

        held = {}

        def x_turn(h, i):
            bank = new_bank()
            words = x_bf[h, i][:].bitcast(F32)
            for q in range(2):
                for u in range(2):
                    s = 2 * q + u
                    nc.tensor.transpose(bank[:, s * P : (s + 1) * P], words[:, 256 * q + u : 256 * (q + 1) : 2], ident[:])
            held["x", h, i] = bank

        def x_out(h, i, engine):
            bank = held.pop(("x", h, i))
            if i == 0:
                t = work.tile([P, 2, 2048], BF16, name="x_grp", bufs=1, align_bytes=64)
                x_grp[h] = t
            copy(
                engine,
                x_grp[h][:].bitcast(F32).rearrange("p q (i r u) -> p i q r u", i=4, u=2)[:, i],
                bank[:].rearrange("p (q u r) -> p q r u", q=2, u=2),
            )

        def x_quant(h, q):
            nc.vector.quantize_mx(out=x_codes[h][:, q, :].bitcast(FP8X4), scales=x_scales[h][:, q, :], in_=x_grp[h][:, q, :])

        w_grp = {}

        def w_ilv(c, q, engine):
            if (c, q) not in w_grp:
                t = work.tile([P, 2048], BF16, name="grp", bufs=8, align_bytes=64)
                w_grp[c, q] = t
            n = W_VEC[c][q]
            t0, t1 = (4 - n, 4) if engine == "v" else (0, 4 - n)
            if t0 < t1:
                copy(
                    engine,
                    w_grp[c, q][:].rearrange("p (t B i s) -> p t B s i", t=4, i=8, s=4)[:, t0:t1],
                    w_raw[c, q][:].rearrange("p s (B t i) -> p t B s i", t=4, i=8)[:, t0:t1],
                )

        def w_quant(c, q):
            nc.vector.quantize_mx(out=w_codes[c][q][:].bitcast(FP8X4), scales=w_scales[c][q][:], in_=w_grp[c, q][:])

        def z_mm(c, h, t):
            bank = new_bank()
            cols = slice(t * P, (t + 1) * P)
            for q in range(2):
                nc.tensor.matmul_mx(
                    out=bank[:],
                    lhsT=w_codes[c][q][:, cols].bitcast(FP8X4),
                    lhsT_scale=w_scales[c][q][:, cols],
                    rhs=x_codes[h][:, q, :].bitcast(FP8X4),
                    rhs_scale=x_scales[h][:, q, :],
                    start=(q == 0),
                    stop=(q == 1),
                )
            held["z", t] = bank

        top = {}

        def z_out(c, h, t):
            group, piece = c // 3, c % 3
            bank = held.pop(("z", t))
            col = bias[:, 4 * c_bias(group, piece) + t : 4 * c_bias(group, piece) + t + 1]
            if t == 0:
                z_piece = work.tile([P, 4, 512], BF16, name=f"z_piece{piece}", align_bytes=64)
                top[h, piece] = z_piece
            if piece == 1:
                nc.vector.scalar_tensor_tensor(out=top[h, 1][:, t, :], in0=bank[:], scalar=col, in1=top[h, 0][:, t, :], op0=ADD, op1=MAX)
            else:
                nc.scalar.activation(out=top[h, piece][:, t, :], in_=bank[:], func=IDENTITY, bias=col)

        def c_bias(group, piece):
            return 2 * piece + group

        h_grp = {}

        def h_max(tiles, group, h, half):
            if half == 0:
                t = work.tile([P, 2048], BF16, name="grp", bufs=8, align_bytes=64)
                h_grp[group, h] = t
            cols = slice(256 * half, 256 * (half + 1))
            nc.vector.tensor_tensor(
                out=h_grp[group, h][:, 1024 * half : 1024 * (half + 1)].rearrange("p (c i t) -> p c t i", i=4, t=4),
                in0=tiles[h, 1][:, :, cols].rearrange("p t (c i) -> p c t i", i=4),
                in1=tiles[h, 2][:, :, cols].rearrange("p t (c i) -> p c t i", i=4),
                op=MAX,
            )

        def h_quant(group, h, half):
            cols = slice(256 * half, 256 * (half + 1))
            nc.vector.quantize_mx(
                out=h_codes[group][h][:, cols].bitcast(FP8X4),
                scales=h_scales[group][h][:, cols],
                in_=h_grp[group, h][:, 1024 * half : 1024 * (half + 1)],
            )

        def e_turn(n):
            bank = new_bank()
            for i in range(2):
                words = e_raw[:, 2 * n + i, :].bitcast(F32)
                for u in range(2):
                    s = 2 * i + u
                    nc.tensor.transpose(bank[:, s * P : (s + 1) * P], words[:, u : 256 : 2], ident[:])
            held["e", n] = bank

        def e_out(n, engine):
            bank = held.pop(("e", n))
            if n % 2 == 0:
                t = work.tile([P, 2048], BF16, name="grp", bufs=8, align_bytes=64)
                e_grp[n // 2] = t
            copy(
                engine,
                e_grp[n // 2][:].bitcast(F32)[:, 512 * (n % 2) : 512 * (n % 2 + 1)].rearrange("p (i r u) -> p i r u", i=2, u=2),
                bank[:].rearrange("p (i u r) -> p i r u", i=2, u=2),
            )

        def e_quant(n):
            nc.vector.quantize_mx(
                out=e_codes[:, 512 * n : 512 * (n + 1)].bitcast(FP8X4),
                scales=e_scales[:, 512 * n : 512 * (n + 1)],
                in_=e_grp[n][:],
            )

        g_grp = {}

        def g_ilv(q, engine):
            if q not in g_grp:
                t = work.tile([P, 2048], BF16, name="grp", bufs=8, align_bytes=64)
                g_grp[q] = t
            n = G_VEC[q]
            t0, t1 = (4 - n, 4) if engine == "v" else (0, 4 - n)
            if t0 < t1:
                copy(
                    engine,
                    g_grp[q][:].rearrange("p (t B i s) -> p t B s i", t=4, i=8, s=4)[:, t0:t1],
                    g_raw[:, :, 512 * q : 512 * (q + 1)].rearrange("p s (B t i) -> p t B s i", t=4, i=8)[:, t0:t1],
                )

        def g_quant(q):
            nc.vector.quantize_mx(out=g_codes[q][:].bitcast(FP8X4), scales=g_scales[q][:], in_=g_grp[q][:])

        v_raw = {}

        def v_mm(q, n, t):
            bank = new_bank()
            cols = slice(t * P, (t + 1) * P)
            rows = slice(512 * n, 512 * (n + 1))
            nc.tensor.matmul_mx(
                out=bank[:],
                lhsT=g_codes[q][:, cols].bitcast(FP8X4),
                lhsT_scale=g_scales[q][:, cols],
                rhs=e_codes[:, rows].bitcast(FP8X4),
                rhs_scale=e_scales[:, rows],
                start=True,
                stop=True,
            )
            held["v", q, n, t] = bank

        def v_out(q, n, t):
            bank = held.pop(("v", q, n, t))
            if t == 0:
                tile = work.tile([P, 4, 512], BF16, name="v_raw", align_bytes=64)
                v_raw[q, n] = tile
            col = bias[:, 24 + 4 * q + t : 25 + 4 * q + t]
            if t in V_OUT_VEC:
                nc.vector.tensor_scalar(out=v_raw[q, n][:, t, :], in0=bank[:], scalar1=col, scalar2=None, op0=ADD)
            else:
                nc.scalar.activation(out=v_raw[q, n][:, t, :], in_=bank[:], func=IDENTITY, bias=col)

        v_grp = {}

        def v_ilv(q, n):
            t = work.tile([P, 2048], BF16, name="grp", bufs=8, align_bytes=64)
            v_grp[q, n] = t
            copy(
                "v" if V_VEC[2 * q + n] else "s",
                t[:].rearrange("p (c i t) -> p c t i", i=8, t=4),
                v_raw[q, n][:].rearrange("p t (c i) -> p c t i", i=8),
            )

        def v_quant(q, n):
            nc.vector.quantize_mx(out=v_codes[q][n][:].bitcast(FP8X4), scales=v_scales[q][n][:], in_=v_grp[q, n][:])

        def y_mm(h, i, n):
            bank = new_bank()
            cols = slice(i * P, (i + 1) * P)
            for q in range(2):
                nc.tensor.matmul_mx(
                    out=bank[:],
                    lhsT=h_codes[q][h][:, cols].bitcast(FP8X4),
                    lhsT_scale=h_scales[q][h][:, cols],
                    rhs=v_codes[q][n][:].bitcast(FP8X4),
                    rhs_scale=v_scales[q][n][:],
                    start=(q == 0),
                    stop=(q == 1),
                )
            held["y", h, i, n] = bank

        out_rows = out.rearrange("(p i) c -> p i c", i=8)

        y_sb = {}

        def y_scale(h, i, n):
            bank = held.pop(("y", h, i, n))
            t = work.tile([P, 512], F32, name="y_sb", bufs=6, align_bytes=64)
            y_sb[h, i, n] = t
            nc.vector.tensor_tensor(out=t[:], in0=bank[:], in1=r_all[:, 512 * n : 512 * (n + 1)], op=MULT)

        def y_store(h, i, n):
            t = y_sb.pop((h, i, n))
            cols = slice(512 * n, 512 * (n + 1))
            engine = nc.gpsimd if ADD_GP[h][i] else nc.vector
            engine.tensor_tensor(out=t[:], in0=t[:], in1=d_all[:, cols], op=ADD)
            nc.sync.dma_start(out=out_rows[:, 4 * h + i, cols], in_=t[:])

        def yt_mm(h, n):
            bank = new_bank()
            cols = slice(n * P, (n + 1) * P)
            for q in range(2):
                nc.tensor.matmul_mx(
                    out=bank[:],
                    lhsT=v_codes[q][1][:, cols].bitcast(FP8X4),
                    lhsT_scale=v_scales[q][1][:, cols],
                    rhs=h_codes[q][h][:].bitcast(FP8X4),
                    rhs_scale=h_scales[q][h][:],
                    start=(q == 0),
                    stop=(q == 1),
                )
            held["yt", h, n] = bank

        def yt_scale(h, n):
            bank = held.pop(("yt", h, n))
            t = work.tile([P, 512], F32, name="yt_sb", bufs=2, align_bytes=64)
            y_sb["t", h, n] = t
            nc.scalar.activation(out=t[:], in_=bank[:], func=IDENTITY, scale=bias[:, 36 + n : 37 + n], bias=bias[:, 44 + n : 45 + n])

        def yt_turn(h, n):
            t = y_sb.pop(("t", h, n))
            bank = new_bank()
            for i in range(4):
                nc.tensor.transpose(bank[:, i * P : (i + 1) * P], t[:, i * P : (i + 1) * P], ident[:])
            held["yr", h, n] = bank

        def yt_store(h, n):
            bank = held.pop(("yr", h, n))
            t = work.tile([P, 512], F32, name="y_turned", bufs=4, align_bytes=64)
            nc.scalar.copy(out=t[:], in_=bank[:])
            nc.sync.dma_start(
                out=out_rows[:, 4 * h : 4 * h + 4, 512 + n * P : 512 + (n + 1) * P],
                in_=t[:].rearrange("p (i c) -> p i c", i=4),
            )

        load_w(1, 0)
        load_w(1, 1)
        x_product(0, 0)
        x_product(0, 1)
        w_ilv(0, 0, "s")
        x_turn(0, 0)
        x_out(0, 0, "s")
        x_product(0, 2)
        x_turn(0, 1)
        x_out(0, 1, "s")
        x_product(0, 3)
        w_ilv(0, 0, "v")
        x_turn(0, 2)
        x_out(0, 2, "s")
        w_ilv(0, 1, "v")
        x_turn(0, 3)
        x_out(0, 3, "s")
        w_ilv(0, 1, "s")
        w_quant(0, 0)
        x_quant(0, 0)
        x_quant(0, 1)
        w_quant(0, 1)
        bias_bank = new_bank()
        nc.tensor.matmul(bias_bank[:, 0:48], lhsT=bias_rows[:], rhs=ident_bf[:, 0:48], start=True, stop=True)
        nc.vector.tensor_copy(out=bias[:], in_=bias_bank[:, 0:48])
        load_w(2, 0)
        load_w(2, 1)
        load_x(1, 0, 4)
        load_w(3, 0)
        load_w(3, 1)
        nc.sync.dma_start(out=e_raw[:], in_=e.rearrange("(i p) k -> p i k", p=P))
        load_w(4, 0)
        load_w(4, 1)
        nc.sync.dma_start(out=g_raw[:], in_=g.rearrange("(p s) f -> p s f", s=4))
        load_w(5, 0)
        load_w(5, 1)
        nc.sync.dma_start(out=r_all[:], in_=r.partition_broadcast(P))
        nc.sync.dma_start(out=d_all[:], in_=d.partition_broadcast(P))

        fill = [[] for s in range(54)]

        def put(s, fn, *args):
            fill[s].append((fn, args))

        for c in range(1, 6):
            s = W_AT[c - 1]
            for q in range(2):
                put(s + q, w_ilv, c, q, "s")
                put(s + q, w_ilv, c, q, "v")
                put(s + q + W_LAG, w_quant, c, q)
        for i in range(4):
            s = X1_AT[i]
            put(s, x_product, 1, i)
            put(s + X_LAG[0], x_turn, 1, i)
            put(s + X_LAG[1], x_out, 1, i, "s")
        for n in range(4):
            put(E_AT + n, e_turn, n)
            put(E_AT + n + 1, e_out, n, "s")
        for q in range(2):
            put(E_AT + 4 + 2 * q, e_quant, q)
            put(X_AT + q, x_quant, 1, q)
            put(G_AT + 2 * q, g_ilv, q, "s")
            put(G_AT + 2 * q, g_ilv, q, "v")
            put(G_AT + 2 * q + 2, g_quant, q)
        for at, (q, n) in enumerate(((0, 0), (1, 0), (0, 1), (1, 1))):
            s = V_AT[at]
            for t in range(4):
                put(s + t // 2, v_mm, q, n, t)
                put(s + t // 2, v_out, q, n, t)
            put(s + 3, v_ilv, q, n)
            put(s + 4, v_quant, q, n)
        for n in range(4):
            put(Y_AT[n], y_mm, 0, n, 0)
            put(Y_AT[n], y_scale, 0, n, 0)
            put(Y_AT[n] + 1, y_store, 0, n, 0)
            put(YT_AT[n], yt_mm, 0, n)
            put(YT_AT[n], yt_scale, 0, n)
            put(YT_AT[n] + 1, yt_turn, 0, n)
            put(YT_AT[n] + 1, yt_store, 0, n)

        for s in range(54):
            t = s % 4
            if s < 48:
                c, h = Z_ORDER[s // 4]
                z_mm(c, h, t)
            for fn, args in fill[s]:
                fn(*args)
            if s < 48:
                z_out(c, h, t)
                if c % 3 == 2 and t == 3:
                    tiles = dict(top)
                    for half in range(2):
                        fill[s + H_LAG[half]].insert(0, (h_max, (tiles, c // 3, h, half)))
                        fill[s + H_LAG[half] + 1].insert(0, (h_quant, (c // 3, h, half)))

        for n in range(6):
            if n < 4:
                y_mm(1, n, 0)
                y_scale(1, n, 0)
            if 0 < n < 5:
                yt_mm(1, n - 1)
                y_store(1, n - 1, 0)
                yt_scale(1, n - 1)
            if n > 1:
                yt_turn(1, n - 2)
                yt_store(1, n - 2)
